import numpy as np
import ml_dtypes


def mxq(x, axis, fmt="e4m3"):
    dtype, down = {"e4m3": (ml_dtypes.float8_e4m3fn, 7), "e5m2": (ml_dtypes.float8_e5m2, 14)}[fmt]
    v = np.moveaxis(np.asarray(x, np.float32).astype(ml_dtypes.bfloat16).astype(np.float64), axis, -1)
    blocks = v.reshape(v.shape[:-1] + (-1, 32))
    amax = np.abs(blocks).max(-1, keepdims=True)
    byte = np.maximum(np.where(amax > 0, np.frexp(amax)[1] - 1 + 127, 0) - down, 1)
    scale = np.exp2(byte - 127.0)
    codes = (blocks / scale).astype(np.float32).astype(dtype).astype(np.float64)
    return np.moveaxis((codes * scale).reshape(v.shape), -1, axis)


WIDE = False


def mx_kscale(k):
    if not WIDE:
        return np.ones(k)
    levels = np.array([10, -10, 5, -5, 0])
    if k % 512:
        return np.exp2(np.random.permutation(np.resize(levels, k // 32))).repeat(32)
    a = np.empty((k // 512, 16))
    for p in range(k // 512):
        a[p, :8] = np.random.permutation(np.resize(levels, 8))
        for g in range(8):
            far = levels[np.abs(levels - a[p, g]) >= 10]
            a[p, g + 8] = far[np.random.randint(len(far))]
    return np.exp2(a.ravel()).repeat(32)


def f64(x):
    return np.asarray(x).astype(np.float64)


def striped(idx):
    return np.tile(np.asarray(idx).reshape(-1, 16).T, (8, 1)).astype(np.uint16)


def unstriped(offs):
    return offs[:16].T.reshape(-1).astype(np.int64)


E2M1 = np.array([0.0, 0.5, 1.0, 1.5, 2.0, 3.0, 4.0, 6.0, -0.0, -0.5, -1.0, -1.5, -2.0, -3.0, -4.0, -6.0])


def pack_weight(w, fmt):
    k, n = w.shape
    w = f64(np.asarray(w, np.float32).astype(ml_dtypes.bfloat16)).reshape(k // 32, 32, n)
    amax = np.abs(w).max(1)
    if fmt == "e4m3":
        byte = np.frexp(amax)[1] - 1 + 127 - 7
    else:
        mant, ex = np.frexp(amax / 6.0)
        byte = np.where(mant > 0.5, ex, ex - 1) + 127
    byte = np.clip(np.where(amax > 0, byte, 1), 1, 254)
    scaled = (w * np.exp2(127.0 - byte)[:, None, :]).reshape(k, n).astype(np.float32)
    by_word = np.ascontiguousarray(scaled.reshape(k // 512, 128, 4, n).transpose(0, 1, 3, 2))
    if fmt == "e4m3":
        words = by_word.astype(ml_dtypes.float8_e4m3fn).view(np.uint8)
    else:
        c = by_word.astype(ml_dtypes.float4_e2m1fn).view(np.uint8) & 0xF
        words = (c[..., 0::2] | (c[..., 1::2] << 4)).reshape(k // 512, 128, 2 * n)
    return np.ascontiguousarray(words), np.ascontiguousarray(byte.astype(np.uint8).reshape(k // 512, 16, n))


def unpack_weight(words, scales, fmt):
    g, _, n = scales.shape
    words = np.ascontiguousarray(words).reshape(g, 128, n, -1)
    if fmt == "e4m3":
        vals = words.view(ml_dtypes.float8_e4m3fn).astype(np.float64)
    else:
        nib = np.empty((g, 128, n, 4), np.uint8)
        nib[..., 0::2] = words & 0xF
        nib[..., 1::2] = words >> 4
        vals = E2M1[nib]
    vals = vals * np.repeat(np.exp2(scales.astype(np.float64) - 127.0), 8, axis=1)[..., None]
    return vals.transpose(0, 1, 3, 2).reshape(g * 512, n)


B, N, T, D, NQ = 1, 512, 2048, 1024, 512


def setup_inputs():
    n = np.random.standard_normal
    idx = np.random.permutation(T)[:B * N]
    s = mx_kscale(D)[:, None]
    kp = pack_weight(n((D, T)) / s, "e2m1")
    return {
        "qT": (n((B, D, NQ)) * s * (0.50 / np.sqrt(D))).astype(np.float32),
        "k_words": np.ascontiguousarray(kp[0].reshape(1, 2, 128, T, 2).transpose(0, 2, 3, 1, 4)).reshape(1, 128, T, 4),
        "k_scales": kp[1],
        "kn": np.tile(np.random.uniform(1.0, 4.0, 2048), (128, 1)).astype(np.float32),
        "bw": np.tile(np.random.uniform(0.1, 0.6, 2048), (128, 1)).astype(np.float32),
        "qn": (np.random.uniform(1.0, 4.0, (B, 1, NQ))).astype(np.float32),
        "offs": striped(idx),
    }


def reference(qT, k_words, k_scales, kn, bw, qn, offs):
    idx = unstriped(offs)
    pick = lambda x, which: x[:, which].reshape(x.shape[0], B, -1).transpose(1, 0, 2)
    k = unpack_weight(k_words.reshape(1, 128, T, 2, 2).transpose(0, 3, 1, 2, 4).reshape(2, 128, 2 * T), k_scales, "e2m1")
    kg = pick(k, idx)
    qq = mxq(f64(qT), 1, "e4m3")
    a = kg.transpose(0, 2, 1) @ qq
    y = np.exp(-np.maximum(pick(f64(kn), idx)[:, :1, :].transpose(0, 2, 1) + f64(qn) - 2.0 * a, 0.0) * pick(f64(bw), idx)[:, :1, :].transpose(0, 2, 1))
    return y

@@ -1,0 +1,177 @@
+from contextlib import ExitStack
+
+import concourse.mybir as mybir
+from concourse.masks import make_identity
+
+F32 = mybir.dt.float32
+BF16 = mybir.dt.bfloat16
+I32 = mybir.dt.int32
+U32 = mybir.dt.uint32
+U16 = mybir.dt.uint16
+U8 = mybir.dt.uint8
+FP8X4 = mybir.dt.float8_e4m3fn_x4
+FP4X4 = mybir.dt.float4_e2m1fn_x4
+ALU = mybir.AluOpType
+ACT = mybir.ActivationFunctionType
+
+P = 128
+SLOTS, POOL, D, NQ = 512, 2048, 1024, 512
+PACK = 4
+K_PASS = P * PACK
+PASSES = D // K_PASS
+SLOT_TILES = SLOTS // P
+N_MM = 128
+CHUNKS = [(0, 256), (256, 256)]
+HALF = SLOTS // 2
+SHIFT = 16
+
+FLOPS = 2 * SLOTS * D * NQ
+BYTES = 4 * D * NQ + 4 * P * POOL + PASSES * 16 * POOL + 2 * 4 * POOL + 4 * NQ + 2 * P * SLOTS // 16 + 4 * SLOTS * NQ
+
+
+def tile_attend_tok_rbf_topk_kernel(tc, qT, k_words, k_scales, kn, bw, qn, offs, out):
+    nc = tc.nc
+    with ExitStack() as ctx:
+        keep = ctx.enter_context(tc.tile_pool(name="keep", bufs=1))
+        psum = ctx.enter_context(tc.psum_pool(name="psum", bufs=1))
+
+        offsets = keep.tile([P, SLOTS // 16], U16, name="offsets")
+        nc.sync.dma_start(offsets[:], offs)
+
+        scale_pool = keep.tile([P, POOL], U8, name="scale_pool", tag="late0", align_bytes=64)
+        nc.gpsimd.memset(scale_pool[:].bitcast(I32), 0)
+        k_sc1 = keep.tile([P, SLOTS], U8, name="k_sc1", align_bytes=64)
+        kn_pool = keep.tile([P, POOL], F32, name="kn_pool", tag="late1", align_bytes=64)
+        bw_pool = keep.tile([P, POOL], F32, name="bw_pool")
+        nc.sync.dma_start(kn_pool[P - 1 : P, :], kn[0:1, :])
+        nc.sync.dma_start(bw_pool[P - 1 : P, :], bw[0:1, :])
+        for r in range(4):
+            nc.sync.dma_start(
+                scale_pool[r:P:SHIFT].bitcast(I32),
+                k_scales[:, r:16:4, :].rearrange("o q t -> q o t").bitcast(I32),
+            )
+        exp_warm = keep.tile([P, 1], F32, name="exp_warm")
+        nc.vector.memset(exp_warm[:], 0.0)
+        exp_warm2 = keep.tile([P, 1], F32, name="exp_warm2")
+        nc.scalar.activation(exp_warm2[:], exp_warm[:], ACT.Exp)
+
+        nc.vector.memset(k_sc1[:].bitcast(I32), 0)
+        nc.vector.memset(kn_pool[0 : P - 1, :].bitcast(I32), 0)
+
+        identity = keep.tile([P, P], F32, name="identity")
+        make_identity(nc, identity[:])
+        nc.gpsimd.memset(bw_pool[0 : P - 1, :].bitcast(I32), 0)
+        qn_cols = keep.tile([P, PACK], F32, name="qn_cols")
+
+        q_rows = qT[0].rearrange("(o p j) w -> o p j w", o=PASSES, j=PACK)
+        word_pool = keep.tile([P, POOL], U32, name="word_pool")
+        q_raw = {}
+
+        def load_q(c, o, tag):
+            c0, w = CHUNKS[c]
+            q_raw[c, o] = keep.tile([P, PACK, w], F32, name="q_raw_%d_%d" % (c, o), tag=tag, align_bytes=64)
+            nc.sync.dma_start(q_raw[c, o][:], q_rows[o][:, :, c0 : c0 + w])
+
+        for o in range(PASSES):
+            load_q(0, o, "early%d" % o)
+        nc.sync.dma_start(word_pool[:].bitcast(I32), k_words[0].rearrange("p t b -> p (t b)").bitcast(I32))
+        nc.scalar.dma_start(qn_cols[:], qn[0, 0].rearrange("(p c) -> p c", c=PACK))
+
+        k_sc0 = keep.tile([P, SLOTS], U8, name="k_sc0", align_bytes=64)
+        nc.vector.tensor_copy(k_sc0[:], scale_pool[:].indirect(offsets[:]))
+        nc.sync.dma_start(k_sc1[0 : P - SHIFT, :].bitcast(I32), k_sc0[SHIFT:P, :].bitcast(I32))
+        k_sc = [k_sc0, k_sc1]
+        load_q(1, 0, "late0")
+        kn_g = keep.tile([P, SLOTS], F32, name="kn_g")
+        nc.vector.tensor_copy(kn_g[:], kn_pool[:].indirect(offsets[:]))
+        load_q(1, 1, "late1")
+        bw_g = keep.tile([P, SLOTS], F32, name="bw_g")
+        nc.vector.tensor_copy(bw_g[:], bw_pool[:].indirect(offsets[:]))
+
+        kn_t = psum.tile([P, SLOT_TILES, P], F32, name="kn_t", tag="bank0")
+        bw_t = psum.tile([P, SLOT_TILES, P], F32, name="bw_t", tag="bank1")
+        qn_t = psum.tile([P, PACK, P], F32, name="qn_t", tag="bank2")
+        for c in range(PACK):
+            nc.tensor.transpose(qn_t[:, c, :], qn_cols[:, c : c + 1].to_broadcast([P, P]), identity[:])
+        for s in range(SLOT_TILES):
+            nc.tensor.transpose(kn_t[:, s, :], kn_g[:, s * P : (s + 1) * P], identity[:])
+        for s in range(SLOT_TILES):
+            nc.tensor.transpose(bw_t[:, s, :], bw_g[:, s * P : (s + 1) * P], identity[:])
+        half_qn = keep.tile([P, NQ], F32, name="half_qn")
+        nc.scalar.mul(half_qn[:].rearrange("p (n c) -> p n c", c=PACK), qn_t[:].rearrange("p c n -> p n c"), 0.5)
+        half_kn = keep.tile([P, SLOT_TILES], F32, name="half_kn")
+        nc.scalar.mul(half_kn[:], kn_t[:, :, P - 1], 0.5)
+        two_bw = keep.tile([P, SLOT_TILES], F32, name="two_bw")
+        nc.scalar.mul(two_bw[:], bw_t[:, :, P - 1], 2.0)
+
+        def cast(c, o):
+            w = CHUNKS[c][1]
+            grouped = keep.tile([P, w * PACK], BF16, name="grouped_%d_%d" % (c, o), align_bytes=64)
+            nc.scalar.copy(
+                grouped[:].rearrange("p (c i j) -> p c j i", i=4, j=PACK),
+                q_raw[c, o][:].rearrange("p j (c i) -> p c j i", i=4),
+            )
+            return grouped
+
+        def quantize(grouped, name):
+            w = grouped.shape[1] // PACK
+            codes = keep.tile([P, w], U32, name=name + "_codes", align_bytes=64)
+            scales = keep.tile([P, w], U8, name=name + "_scales", align_bytes=64)
+            nc.vector.quantize_mx(out=codes[:].bitcast(FP8X4), scales=scales[:], in_=grouped[:])
+            return codes, scales
+
+        quant = {}
+        for o in range(PASSES):
+            quant[0, o] = quantize(cast(0, o), "q_0_%d" % o)
+
+        k_codes = []
+        for h in range(2):
+            pairs = keep.tile([P, HALF], U32, name="pairs_%d" % h)
+            nc.vector.tensor_copy(pairs[:], word_pool[:].indirect(offsets[:, h * HALF // 16 : (h + 1) * HALF // 16]))
+            codes = keep.tile([P, PASSES, 2 * HALF], U8, name="k_codes_%d" % h, align_bytes=64)
+            nc.vector.tensor_copy(codes[:].bitcast(U16), pairs[:].bitcast(U16).rearrange("p (s o) -> p o s", o=PASSES))
+            k_codes.append(codes)
+
+        for o in range(PASSES):
+            quant[1, o] = quantize(cast(1, o), "q_1_%d" % o)
+
+        results = [keep.tile([P, SLOT_TILES, w], F32, name="result_%d" % c) for c, (c0, w) in enumerate(CHUNKS)]
+        units = [(c, s) for c in range(len(CHUNKS)) for s in range(SLOT_TILES)]
+        gaps = {}
+
+        def score(u):
+            c, s = units[u]
+            c0, w = CHUNKS[c]
+            h, sh = divmod(s, 2)
+            acc = psum.tile([P, w], F32, name="acc", tag="bank%d" % ((u + 3) % 8))
+            for n0 in range(0, w, N_MM):
+                for o in range(PASSES):
+                    codes, scales = quant[c, o]
+                    nc.tensor.matmul_mx(
+                        out=acc[:, n0 : n0 + N_MM],
+                        lhsT=k_codes[h][:, o, 2 * sh * P : 2 * (sh + 1) * P].bitcast(FP4X4),
+                        lhsT_scale=k_sc[o][:, s * P : (s + 1) * P],
+                        rhs=codes[:, n0 : n0 + N_MM].bitcast(FP8X4),
+                        rhs_scale=scales[:, n0 : n0 + N_MM],
+                        start=(o == 0),
+                        stop=(o == PASSES - 1),
+                    )
+            gaps[u] = keep.tile([P, w], F32, name="gap_%d" % u)
+            nc.vector.scalar_tensor_tensor(
+                gaps[u][:], acc[:], half_kn[:, s : s + 1], half_qn[:, c0 : c0 + w], ALU.subtract, ALU.subtract
+            )
+
+        def finish(u):
+            c, s = units[u]
+            c0, w = CHUNKS[c]
+            clipped = keep.tile([P, w], F32, name="clipped_%d" % u)
+            nc.vector.tensor_scalar_min(clipped[:], gaps[u][:], 0.0)
+            nc.scalar.activation(results[c][:, s, :], clipped[:], ACT.Exp, scale=two_bw[:, s : s + 1])
+            if s == SLOT_TILES - 1:
+                nc.sync.dma_start(out[0].rearrange("(s p) q -> p s q", p=P)[:, :, c0 : c0 + w], results[c][:])
+
+        score(0)
+        for u in range(1, len(units)):
+            score(u)
+            finish(u - 1)
+        finish(len(units) - 1)

@@ -1,7 +1,6 @@
 from contextlib import ExitStack
 
 import concourse.mybir as mybir
-from concourse.masks import make_identity
 
 F32 = mybir.dt.float32
 BF16 = mybir.dt.bfloat16
@@ -21,9 +20,10 @@ K_PASS = P * PACK
 PASSES = D // K_PASS
 SLOT_TILES = SLOTS // P
 N_MM = 128
-CHUNKS = [(0, 256), (256, 256)]
 HALF = SLOTS // 2
-SHIFT = 16
+QUAD = 32
+BANKS = 8
+CHUNKS = [(0, 256), (256, 128), (384, 128)]
 
 FLOPS = 2 * SLOTS * D * NQ
 BYTES = 4 * D * NQ + 4 * P * POOL + PASSES * 16 * POOL + 2 * 4 * POOL + 4 * NQ + 2 * P * SLOTS // 16 + 4 * SLOTS * NQ
@@ -38,59 +38,72 @@ def tile_attend_tok_rbf_topk_kernel(tc, qT, k_words, k_scales, kn, bw, qn, offs,
         offsets = keep.tile([P, SLOTS // 16], U16, name="offsets")
         nc.sync.dma_start(offsets[:], offs)
 
-        scale_pool = keep.tile([P, POOL], U8, name="scale_pool", tag="late0", align_bytes=64)
-        nc.gpsimd.memset(scale_pool[:].bitcast(I32), 0)
-        k_sc1 = keep.tile([P, SLOTS], U8, name="k_sc1", align_bytes=64)
-        kn_pool = keep.tile([P, POOL], F32, name="kn_pool", tag="late1", align_bytes=64)
-        bw_pool = keep.tile([P, POOL], F32, name="bw_pool")
-        nc.sync.dma_start(kn_pool[P - 1 : P, :], kn[0:1, :])
-        nc.sync.dma_start(bw_pool[P - 1 : P, :], bw[0:1, :])
-        for r in range(4):
-            nc.sync.dma_start(
-                scale_pool[r:P:SHIFT].bitcast(I32),
-                k_scales[:, r:16:4, :].rearrange("o q t -> q o t").bitcast(I32),
-            )
         exp_warm = keep.tile([P, 1], F32, name="exp_warm")
         nc.vector.memset(exp_warm[:], 0.0)
         exp_warm2 = keep.tile([P, 1], F32, name="exp_warm2")
         nc.scalar.activation(exp_warm2[:], exp_warm[:], ACT.Exp)
 
-        nc.vector.memset(k_sc1[:].bitcast(I32), 0)
-        nc.vector.memset(kn_pool[0 : P - 1, :].bitcast(I32), 0)
-
-        identity = keep.tile([P, P], F32, name="identity")
-        make_identity(nc, identity[:])
-        nc.gpsimd.memset(bw_pool[0 : P - 1, :].bitcast(I32), 0)
+        scale_pool = keep.tile([P, POOL // 4], I32, name="scale_pool", tag="scale_pool", align_bytes=64)
+        nc.vector.memset(scale_pool[0 : P - QUAD], 0)
+        nc.sync.dma_start(scale_pool[P - QUAD : P], k_scales.rearrange("o f t -> f o t").bitcast(I32))
+        kn_pool = keep.tile([P, POOL], F32, name="kn_pool", tag="kn_pool", align_bytes=64)
+        bw_pool = keep.tile([P, POOL], F32, name="bw_pool", tag="bw_pool", align_bytes=64)
         qn_cols = keep.tile([P, PACK], F32, name="qn_cols")
+        nc.sync.dma_start(kn_pool[P - 1 : P, :], kn[0:1, :])
+
+        diagonal = keep.tile([P, P], I32, name="diagonal")
+        nc.gpsimd.iota(diagonal[:], pattern=[[-1, P]], base=0, channel_multiplier=1)
+
+        nc.vector.memset(kn_pool[0 : P - 1, :], 0.0)
+        nc.vector.memset(bw_pool[0 : P - 1, :], 0.0)
+        k_sc = keep.tile([P, PASSES, SLOTS], U8, name="k_sc", align_bytes=64)
+        nc.vector.memset(k_sc[:].rearrange("p o s -> p (o s)").bitcast(I32), 0)
+        identity = keep.tile([P, P], F32, name="identity")
+        nc.vector.tensor_scalar(identity[:], diagonal[:], 0.0, None, ALU.is_equal)
 
         q_rows = qT[0].rearrange("(o p j) w -> o p j w", o=PASSES, j=PACK)
+
+        def load_q(o, c0, w, tag):
+            raw = keep.tile([P, PACK, w], F32, name="q_raw_%d_%d" % (o, c0), tag=tag, align_bytes=64)
+            nc.sync.dma_start(raw[:], q_rows[o][:, :, c0 : c0 + w])
+            return raw
+
+        def quantize(raw, name):
+            w = raw.shape[2]
+            grouped = keep.tile([P, w * PACK], BF16, name=name + "_grouped", tag=name + "_grouped", align_bytes=64)
+            nc.scalar.copy(
+                grouped[:].rearrange("p (c i j) -> p c j i", i=4, j=PACK),
+                raw[:].rearrange("p j (c i) -> p c j i", i=4),
+            )
+            codes = keep.tile([P, w], U32, name=name + "_codes", align_bytes=64)
+            scales = keep.tile([P, w], U8, name=name + "_scales", align_bytes=64)
+            nc.vector.quantize_mx(out=codes[:].bitcast(FP8X4), scales=scales[:], in_=grouped[:])
+            return codes, scales
+
+        raw_a = [load_q(0, 0, 256, "raw0")]
+        nc.sync.dma_start(bw_pool[P - 1 : P, :], bw[0:1, :])
+        nc.sync.dma_start(qn_cols[:], qn[0, 0].rearrange("(p c) -> p c", c=PACK))
+        raw_a.append(load_q(1, 0, 256, "raw1"))
         word_pool = keep.tile([P, POOL], U32, name="word_pool")
-        q_raw = {}
-
-        def load_q(c, o, tag):
-            c0, w = CHUNKS[c]
-            q_raw[c, o] = keep.tile([P, PACK, w], F32, name="q_raw_%d_%d" % (c, o), tag=tag, align_bytes=64)
-            nc.sync.dma_start(q_raw[c, o][:], q_rows[o][:, :, c0 : c0 + w])
-
-        for o in range(PASSES):
-            load_q(0, o, "early%d" % o)
         nc.sync.dma_start(word_pool[:].bitcast(I32), k_words[0].rearrange("p t b -> p (t b)").bitcast(I32))
-        nc.scalar.dma_start(qn_cols[:], qn[0, 0].rearrange("(p c) -> p c", c=PACK))
 
-        k_sc0 = keep.tile([P, SLOTS], U8, name="k_sc0", align_bytes=64)
-        nc.vector.tensor_copy(k_sc0[:], scale_pool[:].indirect(offsets[:]))
-        nc.sync.dma_start(k_sc1[0 : P - SHIFT, :].bitcast(I32), k_sc0[SHIFT:P, :].bitcast(I32))
-        k_sc = [k_sc0, k_sc1]
-        load_q(1, 0, "late0")
+        scale_rows = keep.tile([P, SLOTS], U8, name="scale_rows", align_bytes=64)
+        nc.vector.tensor_copy(scale_rows[:], scale_pool[:].bitcast(U8).indirect(offsets[:]))
+        for quad in range(P // QUAD):
+            p0 = QUAD * quad
+            nc.sync.dma_start(
+                k_sc[p0 : p0 + 4].rearrange("p o s -> p (o s)").bitcast(I32),
+                scale_rows[P - QUAD + 8 * quad : P - QUAD + 8 * (quad + 1), :].bitcast(I32),
+            )
+        raw_bc0 = load_q(0, 256, 256, "scale_pool")
         kn_g = keep.tile([P, SLOTS], F32, name="kn_g")
         nc.vector.tensor_copy(kn_g[:], kn_pool[:].indirect(offsets[:]))
-        load_q(1, 1, "late1")
         bw_g = keep.tile([P, SLOTS], F32, name="bw_g")
         nc.vector.tensor_copy(bw_g[:], bw_pool[:].indirect(offsets[:]))
 
-        kn_t = psum.tile([P, SLOT_TILES, P], F32, name="kn_t", tag="bank0")
-        bw_t = psum.tile([P, SLOT_TILES, P], F32, name="bw_t", tag="bank1")
-        qn_t = psum.tile([P, PACK, P], F32, name="qn_t", tag="bank2")
+        qn_t = psum.tile([P, PACK, P], F32, name="qn_t", tag="bank5")
+        kn_t = psum.tile([P, SLOT_TILES, P], F32, name="kn_t", tag="bank6")
+        bw_t = psum.tile([P, SLOT_TILES, P], F32, name="bw_t", tag="bank7")
         for c in range(PACK):
             nc.tensor.transpose(qn_t[:, c, :], qn_cols[:, c : c + 1].to_broadcast([P, P]), identity[:])
         for s in range(SLOT_TILES):
@@ -99,30 +112,14 @@ def tile_attend_tok_rbf_topk_kernel(tc, qT, k_words, k_scales, kn, bw, qn, offs,
             nc.tensor.transpose(bw_t[:, s, :], bw_g[:, s * P : (s + 1) * P], identity[:])
         half_qn = keep.tile([P, NQ], F32, name="half_qn")
         nc.scalar.mul(half_qn[:].rearrange("p (n c) -> p n c", c=PACK), qn_t[:].rearrange("p c n -> p n c"), 0.5)
+
+        quant_a = [quantize(raw_a[o], "a%d" % o) for o in range(PASSES)]
+        raw_b1 = load_q(1, 256, 128, "kn_pool")
+        raw_c1 = load_q(1, 384, 128, "bw_pool")
         half_kn = keep.tile([P, SLOT_TILES], F32, name="half_kn")
         nc.scalar.mul(half_kn[:], kn_t[:, :, P - 1], 0.5)
         two_bw = keep.tile([P, SLOT_TILES], F32, name="two_bw")
         nc.scalar.mul(two_bw[:], bw_t[:, :, P - 1], 2.0)
-
-        def cast(c, o):
-            w = CHUNKS[c][1]
-            grouped = keep.tile([P, w * PACK], BF16, name="grouped_%d_%d" % (c, o), align_bytes=64)
-            nc.scalar.copy(
-                grouped[:].rearrange("p (c i j) -> p c j i", i=4, j=PACK),
-                q_raw[c, o][:].rearrange("p j (c i) -> p c j i", i=4),
-            )
-            return grouped
-
-        def quantize(grouped, name):
-            w = grouped.shape[1] // PACK
-            codes = keep.tile([P, w], U32, name=name + "_codes", align_bytes=64)
-            scales = keep.tile([P, w], U8, name=name + "_scales", align_bytes=64)
-            nc.vector.quantize_mx(out=codes[:].bitcast(FP8X4), scales=scales[:], in_=grouped[:])
-            return codes, scales
-
-        quant = {}
-        for o in range(PASSES):
-            quant[0, o] = quantize(cast(0, o), "q_0_%d" % o)
 
         k_codes = []
         for h in range(2):
@@ -132,31 +129,39 @@ def tile_attend_tok_rbf_topk_kernel(tc, qT, k_words, k_scales, kn, bw, qn, offs,
             nc.vector.tensor_copy(codes[:].bitcast(U16), pairs[:].bitcast(U16).rearrange("p (s o) -> p o s", o=PASSES))
             k_codes.append(codes)
 
-        for o in range(PASSES):
-            quant[1, o] = quantize(cast(1, o), "q_1_%d" % o)
+        quant_bc0 = quantize(raw_bc0, "bc0")
+        quant_b1 = quantize(raw_b1, "b1")
+        quant_c1 = quantize(raw_c1, "c1")
+        operands = [
+            [(quant_a[0], 0), (quant_a[1], 0)],
+            [(quant_bc0, 0), (quant_b1, 0)],
+            [(quant_bc0, 128), (quant_c1, 0)],
+        ]
 
         results = [keep.tile([P, SLOT_TILES, w], F32, name="result_%d" % c) for c, (c0, w) in enumerate(CHUNKS)]
         units = [(c, s) for c in range(len(CHUNKS)) for s in range(SLOT_TILES)]
+        out_tiles = out[0].rearrange("(s p) q -> p s q", p=P)
         gaps = {}
+        gap_tags = {1: "bc0_grouped", 2: "b1_grouped", 3: "c1_grouped"}
 
         def score(u):
             c, s = units[u]
             c0, w = CHUNKS[c]
             h, sh = divmod(s, 2)
-            acc = psum.tile([P, w], F32, name="acc", tag="bank%d" % ((u + 3) % 8))
+            acc = psum.tile([P, w], F32, name="acc", tag="bank%d" % (u % BANKS))
             for n0 in range(0, w, N_MM):
                 for o in range(PASSES):
-                    codes, scales = quant[c, o]
+                    (codes, scales), base = operands[c][o]
                     nc.tensor.matmul_mx(
                         out=acc[:, n0 : n0 + N_MM],
                         lhsT=k_codes[h][:, o, 2 * sh * P : 2 * (sh + 1) * P].bitcast(FP4X4),
-                        lhsT_scale=k_sc[o][:, s * P : (s + 1) * P],
-                        rhs=codes[:, n0 : n0 + N_MM].bitcast(FP8X4),
-                        rhs_scale=scales[:, n0 : n0 + N_MM],
+                        lhsT_scale=k_sc[:, o, s * P : (s + 1) * P],
+                        rhs=codes[:, base + n0 : base + n0 + N_MM].bitcast(FP8X4),
+                        rhs_scale=scales[:, base + n0 : base + n0 + N_MM],
                         start=(o == 0),
                         stop=(o == PASSES - 1),
                     )
-            gaps[u] = keep.tile([P, w], F32, name="gap_%d" % u)
+            gaps[u] = keep.tile([P, w], F32, name="gap_%d" % u, tag=gap_tags.get(u, "gap_%d" % u), align_bytes=64)
             nc.vector.scalar_tensor_tensor(
                 gaps[u][:], acc[:], half_kn[:, s : s + 1], half_qn[:, c0 : c0 + w], ALU.subtract, ALU.subtract
             )
@@ -167,8 +172,10 @@ def tile_attend_tok_rbf_topk_kernel(tc, qT, k_words, k_scales, kn, bw, qn, offs,
             clipped = keep.tile([P, w], F32, name="clipped_%d" % u)
             nc.vector.tensor_scalar_min(clipped[:], gaps[u][:], 0.0)
             nc.scalar.activation(results[c][:, s, :], clipped[:], ACT.Exp, scale=two_bw[:, s : s + 1])
-            if s == SLOT_TILES - 1:
-                nc.sync.dma_start(out[0].rearrange("(s p) q -> p s q", p=P)[:, :, c0 : c0 + w], results[c][:])
+            tiles_a_store = 2 if c == len(CHUNKS) - 1 else SLOT_TILES
+            if (s + 1) % tiles_a_store == 0:
+                s0 = s + 1 - tiles_a_store
+                nc.sync.dma_start(out_tiles[:, s0 : s + 1, c0 : c0 + w], results[c][:, s0 : s + 1, :])
 
         score(0)
         for u in range(1, len(units)):

@@ -110,16 +110,16 @@ def tile_attend_tok_rbf_topk_kernel(tc, qT, k_words, k_scales, kn, bw, qn, offs,
             nc.tensor.transpose(kn_t[:, s, :], kn_g[:, s * P : (s + 1) * P], identity[:])
         for s in range(SLOT_TILES):
             nc.tensor.transpose(bw_t[:, s, :], bw_g[:, s * P : (s + 1) * P], identity[:])
-        half_qn = keep.tile([P, NQ], F32, name="half_qn")
-        nc.scalar.mul(half_qn[:].rearrange("p (n c) -> p n c", c=PACK), qn_t[:].rearrange("p c n -> p n c"), 0.5)
-
         quant_a = [quantize(raw_a[o], "a%d" % o) for o in range(PASSES)]
         raw_b1 = load_q(1, 256, 128, "kn_pool")
         raw_c1 = load_q(1, 384, 128, "bw_pool")
-        half_kn = keep.tile([P, SLOT_TILES], F32, name="half_kn")
-        nc.scalar.mul(half_kn[:], kn_t[:, :, P - 1], 0.5)
-        two_bw = keep.tile([P, SLOT_TILES], F32, name="two_bw")
-        nc.scalar.mul(two_bw[:], bw_t[:, :, P - 1], 2.0)
+        terms = keep.tile([P, NQ + 2 * SLOT_TILES], F32, name="terms", tag="raw1", align_bytes=64)
+        half_qn = terms[:, 0:NQ]
+        half_kn = terms[:, NQ : NQ + SLOT_TILES]
+        two_bw = terms[:, NQ + SLOT_TILES :]
+        nc.scalar.mul(half_qn.rearrange("p (n c) -> p n c", c=PACK), qn_t[:].rearrange("p c n -> p n c"), 0.5)
+        nc.scalar.mul(half_kn, kn_t[:, :, P - 1], 0.5)
+        nc.scalar.mul(two_bw, bw_t[:, :, P - 1], -2.0)
 
         k_codes = []
         for h in range(2):
@@ -142,7 +142,7 @@ def tile_attend_tok_rbf_topk_kernel(tc, qT, k_words, k_scales, kn, bw, qn, offs,
         units = [(c, s) for c in range(len(CHUNKS)) for s in range(SLOT_TILES)]
         out_tiles = out[0].rearrange("(s p) q -> p s q", p=P)
         gaps = {}
-        gap_tags = {1: "bc0_grouped", 2: "b1_grouped", 3: "c1_grouped"}
+        gap_tags = {1: "bc0_grouped", 2: "b1_grouped", 4: "c1_grouped"}
 
         def score(u):
             c, s = units[u]
@@ -170,12 +170,16 @@ def tile_attend_tok_rbf_topk_kernel(tc, qT, k_words, k_scales, kn, bw, qn, offs,
             c, s = units[u]
             c0, w = CHUNKS[c]
             clipped = keep.tile([P, w], F32, name="clipped_%d" % u)
-            nc.vector.tensor_scalar_min(clipped[:], gaps[u][:], 0.0)
+            if c == 1:
+                nc.scalar.activation(clipped[:], gaps[u][:], ACT.Relu, scale=-1.0)
+            else:
+                nc.vector.tensor_scalar(clipped[:], gaps[u][:], 0.0, -1.0, ALU.min, ALU.mult)
             nc.scalar.activation(results[c][:, s, :], clipped[:], ACT.Exp, scale=two_bw[:, s : s + 1])
-            tiles_a_store = 2 if c == len(CHUNKS) - 1 else SLOT_TILES
+            tiles_a_store = 2
             if (s + 1) % tiles_a_store == 0:
                 s0 = s + 1 - tiles_a_store
-                nc.sync.dma_start(out_tiles[:, s0 : s + 1, c0 : c0 + w], results[c][:, s0 : s + 1, :])
+                queue = nc.scalar if u == len(units) - 1 else nc.sync
+                queue.dma_start(out_tiles[:, s0 : s + 1, c0 : c0 + w], results[c][:, s0 : s + 1, :])
 
         score(0)
         for u in range(1, len(units)):

@@ -16,14 +16,19 @@ ACT = mybir.ActivationFunctionType
 P = 128
 SLOTS, POOL, D, NQ = 512, 2048, 1024, 512
 PACK = 4
-K_PASS = P * PACK
-PASSES = D // K_PASS
+PASSES = D // (P * PACK)
 SLOT_TILES = SLOTS // P
-N_MM = 128
 HALF = SLOTS // 2
 QUAD = 32
+SCALE_ROWS = 4
+LIST_ROWS = 16
+N_MM = 128
 BANKS = 8
+LINE = 4
+TILES_A_STORE = 2
+
 CHUNKS = [(0, 256), (256, 128), (384, 128)]
+SCALAR_CLIP_CHUNK = 1
 
 FLOPS = 2 * SLOTS * D * NQ
 BYTES = 4 * D * NQ + 4 * P * POOL + PASSES * 16 * POOL + 2 * 4 * POOL + 4 * NQ + 2 * P * SLOTS // 16 + 4 * SLOTS * NQ
@@ -35,151 +40,177 @@ def tile_attend_tok_rbf_topk_kernel(tc, qT, k_words, k_scales, kn, bw, qn, offs,
         keep = ctx.enter_context(tc.tile_pool(name="keep", bufs=1))
         psum = ctx.enter_context(tc.psum_pool(name="psum", bufs=1))
 
-        offsets = keep.tile([P, SLOTS // 16], U16, name="offsets")
+        offsets = keep.tile([P, SLOTS // LIST_ROWS], U16, name="offsets")
         nc.sync.dma_start(offsets[:], offs)
 
-        exp_warm = keep.tile([P, 1], F32, name="exp_warm")
-        nc.vector.memset(exp_warm[:], 0.0)
-        exp_warm2 = keep.tile([P, 1], F32, name="exp_warm2")
-        nc.scalar.activation(exp_warm2[:], exp_warm[:], ACT.Exp)
+        zero = keep.tile([P, 1], F32, name="zero", tag="zero", align_bytes=64)
+        nc.vector.memset(zero[:], 0.0)
+        one = keep.tile([P, 1], F32, name="one")
+        nc.scalar.activation(one[:], zero[:], ACT.Exp)
 
         scale_pool = keep.tile([P, POOL // 4], I32, name="scale_pool", tag="scale_pool", align_bytes=64)
         nc.vector.memset(scale_pool[0 : P - QUAD], 0)
         nc.sync.dma_start(scale_pool[P - QUAD : P], k_scales.rearrange("o f t -> f o t").bitcast(I32))
         kn_pool = keep.tile([P, POOL], F32, name="kn_pool", tag="kn_pool", align_bytes=64)
         bw_pool = keep.tile([P, POOL], F32, name="bw_pool", tag="bw_pool", align_bytes=64)
-        qn_cols = keep.tile([P, PACK], F32, name="qn_cols")
         nc.sync.dma_start(kn_pool[P - 1 : P, :], kn[0:1, :])
+        nc.vector.memset(kn_pool[0 : P - 1, :].bitcast(I32), 0)
+        nc.vector.memset(bw_pool[0 : P - 1, :].bitcast(I32), 0)
 
-        diagonal = keep.tile([P, P], I32, name="diagonal")
-        nc.gpsimd.iota(diagonal[:], pattern=[[-1, P]], base=0, channel_multiplier=1)
+        k_scale = keep.tile([P, PASSES, SLOTS], U8, name="k_scale", align_bytes=64)
+        nc.vector.memset(k_scale[:].rearrange("p o s -> p (o s)").bitcast(I32), 0)
 
-        nc.vector.memset(kn_pool[0 : P - 1, :], 0.0)
-        nc.vector.memset(bw_pool[0 : P - 1, :], 0.0)
-        k_sc = keep.tile([P, PASSES, SLOTS], U8, name="k_sc", align_bytes=64)
-        nc.vector.memset(k_sc[:].rearrange("p o s -> p (o s)").bitcast(I32), 0)
+        row_minus_column = keep.tile([P, P], I32, name="row_minus_column")
+        nc.gpsimd.iota(row_minus_column[:], pattern=[[-1, P]], base=0, channel_multiplier=1)
         identity = keep.tile([P, P], F32, name="identity")
-        nc.vector.tensor_scalar(identity[:], diagonal[:], 0.0, None, ALU.is_equal)
+        nc.vector.tensor_scalar(identity[:], row_minus_column[:], 0.0, one[:], ALU.is_equal, ALU.mult)
 
         q_rows = qT[0].rearrange("(o p j) w -> o p j w", o=PASSES, j=PACK)
 
-        def load_q(o, c0, w, tag):
-            raw = keep.tile([P, PACK, w], F32, name="q_raw_%d_%d" % (o, c0), tag=tag, align_bytes=64)
-            nc.sync.dma_start(raw[:], q_rows[o][:, :, c0 : c0 + w])
+        def load_q(o, c0, width, tag):
+            raw = keep.tile([P, PACK, width], F32, name="raw_%d_%d" % (o, c0), tag=tag, align_bytes=64)
+            nc.sync.dma_start(raw[:], q_rows[o][:, :, c0 : c0 + width])
             return raw
 
-        def quantize(raw, name):
-            w = raw.shape[2]
-            grouped = keep.tile([P, w * PACK], BF16, name=name + "_grouped", tag=name + "_grouped", align_bytes=64)
+        def quantize(raw, name, tag):
+            width = raw.shape[2]
+            grouped = keep.tile([P, width * PACK], BF16, name=name + "_grouped", tag=tag, align_bytes=64)
             nc.scalar.copy(
-                grouped[:].rearrange("p (c i j) -> p c j i", i=4, j=PACK),
-                raw[:].rearrange("p j (c i) -> p c j i", i=4),
+                grouped[:].rearrange("p (c i j) -> p c j i", i=LINE, j=PACK),
+                raw[:].rearrange("p j (c i) -> p c j i", i=LINE),
             )
-            codes = keep.tile([P, w], U32, name=name + "_codes", align_bytes=64)
-            scales = keep.tile([P, w], U8, name=name + "_scales", align_bytes=64)
+            codes = keep.tile([P, width], U32, name=name + "_codes", align_bytes=64)
+            scales = keep.tile([P, width], U8, name=name + "_scales", align_bytes=64)
             nc.vector.quantize_mx(out=codes[:].bitcast(FP8X4), scales=scales[:], in_=grouped[:])
             return codes, scales
 
-        raw_a = [load_q(0, 0, 256, "raw0")]
+        (first0, first_width), (second0, second_width), (third0, third_width) = CHUNKS
+
+        raw_first = [load_q(0, first0, first_width, "raw_first0")]
         nc.sync.dma_start(bw_pool[P - 1 : P, :], bw[0:1, :])
+        qn_cols = keep.tile([P, PACK], F32, name="qn_cols")
         nc.sync.dma_start(qn_cols[:], qn[0, 0].rearrange("(p c) -> p c", c=PACK))
-        raw_a.append(load_q(1, 0, 256, "raw1"))
+        raw_first.append(load_q(1, first0, first_width, "raw_first1"))
         word_pool = keep.tile([P, POOL], U32, name="word_pool")
         nc.sync.dma_start(word_pool[:].bitcast(I32), k_words[0].rearrange("p t b -> p (t b)").bitcast(I32))
 
         scale_rows = keep.tile([P, SLOTS], U8, name="scale_rows", align_bytes=64)
         nc.vector.tensor_copy(scale_rows[:], scale_pool[:].bitcast(U8).indirect(offsets[:]))
+        rows_a_quad = PASSES * SCALE_ROWS
         for quad in range(P // QUAD):
-            p0 = QUAD * quad
+            source = P - QUAD + rows_a_quad * quad
             nc.sync.dma_start(
-                k_sc[p0 : p0 + 4].rearrange("p o s -> p (o s)").bitcast(I32),
-                scale_rows[P - QUAD + 8 * quad : P - QUAD + 8 * (quad + 1), :].bitcast(I32),
+                k_scale[QUAD * quad : QUAD * quad + SCALE_ROWS].rearrange("p o s -> p (o s)").bitcast(I32),
+                scale_rows[source : source + rows_a_quad, :].bitcast(I32),
             )
-        raw_bc0 = load_q(0, 256, 256, "scale_pool")
-        kn_g = keep.tile([P, SLOTS], F32, name="kn_g")
-        nc.vector.tensor_copy(kn_g[:], kn_pool[:].indirect(offsets[:]))
-        bw_g = keep.tile([P, SLOTS], F32, name="bw_g")
-        nc.vector.tensor_copy(bw_g[:], bw_pool[:].indirect(offsets[:]))
+        kn_listed = keep.tile([P, SLOTS], F32, name="kn_listed")
+        nc.vector.tensor_copy(kn_listed[:], kn_pool[:].indirect(offsets[:]))
+        bw_listed = keep.tile([P, SLOTS], F32, name="bw_listed")
+        nc.vector.tensor_copy(bw_listed[:], bw_pool[:].indirect(offsets[:]))
 
-        qn_t = psum.tile([P, PACK, P], F32, name="qn_t", tag="bank5")
-        kn_t = psum.tile([P, SLOT_TILES, P], F32, name="kn_t", tag="bank6")
-        bw_t = psum.tile([P, SLOT_TILES, P], F32, name="bw_t", tag="bank7")
+        raw_rest0 = load_q(0, second0, second_width + third_width, "scale_pool")
+        raw_second1 = load_q(1, second0, second_width, "kn_pool")
+        raw_third1 = load_q(1, third0, third_width, "bw_pool")
+
+        qn_t = psum.tile([P, PACK, P], F32, name="qn_t", tag="bank%d" % (BANKS - 3))
+        kn_t = psum.tile([P, SLOT_TILES, P], F32, name="kn_t", tag="bank%d" % (BANKS - 2))
+        bw_t = psum.tile([P, SLOT_TILES, P], F32, name="bw_t", tag="bank%d" % (BANKS - 1))
         for c in range(PACK):
             nc.tensor.transpose(qn_t[:, c, :], qn_cols[:, c : c + 1].to_broadcast([P, P]), identity[:])
         for s in range(SLOT_TILES):
-            nc.tensor.transpose(kn_t[:, s, :], kn_g[:, s * P : (s + 1) * P], identity[:])
+            nc.tensor.transpose(kn_t[:, s, :], kn_listed[:, s * P : (s + 1) * P], identity[:])
         for s in range(SLOT_TILES):
-            nc.tensor.transpose(bw_t[:, s, :], bw_g[:, s * P : (s + 1) * P], identity[:])
-        quant_a = [quantize(raw_a[o], "a%d" % o) for o in range(PASSES)]
-        raw_b1 = load_q(1, 256, 128, "kn_pool")
-        raw_c1 = load_q(1, 384, 128, "bw_pool")
-        terms = keep.tile([P, NQ + 2 * SLOT_TILES], F32, name="terms", tag="raw1", align_bytes=64)
+            nc.tensor.transpose(bw_t[:, s, :], bw_listed[:, s * P : (s + 1) * P], identity[:])
+
+        q_first = [quantize(raw_first[o], "first%d" % o, "first%d_grouped" % o) for o in range(PASSES)]
+
+        terms = keep.tile([P, NQ + 2 * SLOT_TILES], F32, name="terms", tag="raw_first1", align_bytes=64)
         half_qn = terms[:, 0:NQ]
         half_kn = terms[:, NQ : NQ + SLOT_TILES]
-        two_bw = terms[:, NQ + SLOT_TILES :]
-        nc.scalar.mul(half_qn.rearrange("p (n c) -> p n c", c=PACK), qn_t[:].rearrange("p c n -> p n c"), 0.5)
-        nc.scalar.mul(half_kn, kn_t[:, :, P - 1], 0.5)
-        nc.scalar.mul(two_bw, bw_t[:, :, P - 1], -2.0)
+        minus_two_bw = terms[:, NQ + SLOT_TILES :]
+        nc.scalar.activation(
+            half_qn.rearrange("p (n c) -> p n c", c=PACK),
+            qn_t[:].rearrange("p c n -> p n c"),
+            ACT.Identity,
+            bias=zero[:],
+            scale=0.5,
+        )
+        nc.scalar.activation(half_kn, kn_t[:, :, P - 1], ACT.Identity, bias=zero[:], scale=0.5)
+        nc.scalar.activation(minus_two_bw, bw_t[:, :, P - 1], ACT.Identity, bias=zero[:], scale=-2.0)
 
         k_codes = []
-        for h in range(2):
+        for h in range(SLOTS // HALF):
             pairs = keep.tile([P, HALF], U32, name="pairs_%d" % h)
-            nc.vector.tensor_copy(pairs[:], word_pool[:].indirect(offsets[:, h * HALF // 16 : (h + 1) * HALF // 16]))
-            codes = keep.tile([P, PASSES, 2 * HALF], U8, name="k_codes_%d" % h, align_bytes=64)
-            nc.vector.tensor_copy(codes[:].bitcast(U16), pairs[:].bitcast(U16).rearrange("p (s o) -> p o s", o=PASSES))
-            k_codes.append(codes)
+            entries = offsets[:, h * HALF // LIST_ROWS : (h + 1) * HALF // LIST_ROWS]
+            nc.vector.tensor_copy(pairs[:], word_pool[:].indirect(entries))
+            parted = keep.tile([P, PASSES, 2 * HALF], U8, name="k_codes_%d" % h, align_bytes=64)
+            nc.vector.tensor_copy(parted[:].bitcast(U16), pairs[:].bitcast(U16).rearrange("p (s o) -> p o s", o=PASSES))
+            k_codes.append(parted)
 
-        quant_bc0 = quantize(raw_bc0, "bc0")
-        quant_b1 = quantize(raw_b1, "b1")
-        quant_c1 = quantize(raw_c1, "c1")
-        operands = [
-            [(quant_a[0], 0), (quant_a[1], 0)],
-            [(quant_bc0, 0), (quant_b1, 0)],
-            [(quant_bc0, 128), (quant_c1, 0)],
+        q_rest0 = quantize(raw_rest0, "rest0", "zero")
+        q_second1 = quantize(raw_second1, "second1", "scale_pool")
+        q_third1 = quantize(raw_third1, "third1", "kn_pool")
+        moving = [
+            [(q_first[0], 0), (q_first[1], 0)],
+            [(q_rest0, 0), (q_second1, 0)],
+            [(q_rest0, second_width), (q_third1, 0)],
         ]
 
-        results = [keep.tile([P, SLOT_TILES, w], F32, name="result_%d" % c) for c, (c0, w) in enumerate(CHUNKS)]
+        result_tags = ["bw_pool", "result_second", "result_third"]
+        results = [
+            keep.tile([P, SLOT_TILES, width], F32, name="result_%d" % c, tag=result_tags[c], align_bytes=64)
+            for c, (c0, width) in enumerate(CHUNKS)
+        ]
+        first_tags = ["gap_first0", "zero", "scale_pool", "gap_first3"]
+        gaps_first = [
+            keep.tile([P, first_width], F32, name="gap_first%d" % s, tag=first_tags[s], align_bytes=64)
+            for s in range(SLOT_TILES)
+        ]
+        gaps_second = keep.tile([P, SLOT_TILES, second_width], F32, name="gaps_second", tag="kn_pool", align_bytes=64)
+        gaps_third = keep.tile([P, SLOT_TILES, third_width], F32, name="gaps_third")
+        gaps = [
+            [tile[:] for tile in gaps_first],
+            [gaps_second[:, s, :] for s in range(SLOT_TILES)],
+            [gaps_third[:, s, :] for s in range(SLOT_TILES)],
+        ]
+
         units = [(c, s) for c in range(len(CHUNKS)) for s in range(SLOT_TILES)]
         out_tiles = out[0].rearrange("(s p) q -> p s q", p=P)
-        gaps = {}
-        gap_tags = {1: "bc0_grouped", 2: "b1_grouped", 4: "c1_grouped"}
 
         def score(u):
             c, s = units[u]
-            c0, w = CHUNKS[c]
-            h, sh = divmod(s, 2)
-            acc = psum.tile([P, w], F32, name="acc", tag="bank%d" % (u % BANKS))
-            for n0 in range(0, w, N_MM):
+            c0, width = CHUNKS[c]
+            h, tile_in_half = divmod(s, HALF // P)
+            acc = psum.tile([P, width], F32, name="acc", tag="bank%d" % (u % BANKS))
+            for n0 in range(0, width, N_MM):
                 for o in range(PASSES):
-                    (codes, scales), base = operands[c][o]
+                    (codes, scales), base = moving[c][o]
                     nc.tensor.matmul_mx(
                         out=acc[:, n0 : n0 + N_MM],
-                        lhsT=k_codes[h][:, o, 2 * sh * P : 2 * (sh + 1) * P].bitcast(FP4X4),
-                        lhsT_scale=k_sc[:, o, s * P : (s + 1) * P],
+                        lhsT=k_codes[h][:, o, 2 * tile_in_half * P : 2 * (tile_in_half + 1) * P].bitcast(FP4X4),
+                        lhsT_scale=k_scale[:, o, s * P : (s + 1) * P],
                         rhs=codes[:, base + n0 : base + n0 + N_MM].bitcast(FP8X4),
                         rhs_scale=scales[:, base + n0 : base + n0 + N_MM],
                         start=(o == 0),
                         stop=(o == PASSES - 1),
                     )
-            gaps[u] = keep.tile([P, w], F32, name="gap_%d" % u, tag=gap_tags.get(u, "gap_%d" % u), align_bytes=64)
             nc.vector.scalar_tensor_tensor(
-                gaps[u][:], acc[:], half_kn[:, s : s + 1], half_qn[:, c0 : c0 + w], ALU.subtract, ALU.subtract
+                gaps[c][s], acc[:], half_kn[:, s : s + 1], half_qn[:, c0 : c0 + width], ALU.subtract, ALU.subtract
             )
 
         def finish(u):
             c, s = units[u]
-            c0, w = CHUNKS[c]
-            clipped = keep.tile([P, w], F32, name="clipped_%d" % u)
-            if c == 1:
-                nc.scalar.activation(clipped[:], gaps[u][:], ACT.Relu, scale=-1.0)
+            c0, width = CHUNKS[c]
+            clipped = keep.tile([P, width], F32, name="clipped_%d" % u)
+            if c == SCALAR_CLIP_CHUNK:
+                nc.scalar.activation(clipped[:], gaps[c][s], ACT.Relu, scale=-1.0)
             else:
-                nc.vector.tensor_scalar(clipped[:], gaps[u][:], 0.0, -1.0, ALU.min, ALU.mult)
-            nc.scalar.activation(results[c][:, s, :], clipped[:], ACT.Exp, scale=two_bw[:, s : s + 1])
-            tiles_a_store = 2
-            if (s + 1) % tiles_a_store == 0:
-                s0 = s + 1 - tiles_a_store
+                nc.vector.tensor_scalar(clipped[:], gaps[c][s], 0.0, -1.0, ALU.min, ALU.mult)
+            nc.scalar.activation(results[c][:, s, :], clipped[:], ACT.Exp, scale=minus_two_bw[:, s : s + 1])
+            if (s + 1) % TILES_A_STORE == 0:
+                s0 = s + 1 - TILES_A_STORE
                 queue = nc.scalar if u == len(units) - 1 else nc.sync
-                queue.dma_start(out_tiles[:, s0 : s + 1, c0 : c0 + w], results[c][:, s0 : s + 1, :])
+                queue.dma_start(out_tiles[:, s0 : s + 1, c0 : c0 + width], results[c][:, s0 : s + 1, :])
 
         score(0)
         for u in range(1, len(units)):

from contextlib import ExitStack

import concourse.mybir as mybir

F32 = mybir.dt.float32
BF16 = mybir.dt.bfloat16
I32 = mybir.dt.int32
U32 = mybir.dt.uint32
U16 = mybir.dt.uint16
U8 = mybir.dt.uint8
FP8X4 = mybir.dt.float8_e4m3fn_x4
FP4X4 = mybir.dt.float4_e2m1fn_x4
ALU = mybir.AluOpType
ACT = mybir.ActivationFunctionType

P = 128
SLOTS, POOL, D, NQ = 512, 2048, 1024, 512
PACK = 4
PASSES = D // (P * PACK)
SLOT_TILES = SLOTS // P
HALF = SLOTS // 2
QUAD = 32
SCALE_ROWS = 4
LIST_ROWS = 16
N_MM = 128
BANKS = 8
LINE = 4
TILES_A_STORE = 2

CHUNKS = [(0, 256), (256, 128), (384, 128)]
SCALAR_CLIP_CHUNK = 1

FLOPS = 2 * SLOTS * D * NQ
BYTES = 4 * D * NQ + 4 * P * POOL + PASSES * 16 * POOL + 2 * 4 * POOL + 4 * NQ + 2 * P * SLOTS // 16 + 4 * SLOTS * NQ


def tile_attend_tok_rbf_topk_kernel(tc, qT, k_words, k_scales, kn, bw, qn, offs, out):
    nc = tc.nc
    with ExitStack() as ctx:
        keep = ctx.enter_context(tc.tile_pool(name="keep", bufs=1))
        psum = ctx.enter_context(tc.psum_pool(name="psum", bufs=1))

        offsets = keep.tile([P, SLOTS // LIST_ROWS], U16, name="offsets")
        nc.sync.dma_start(offsets[:], offs)

        zero = keep.tile([P, 1], F32, name="zero", tag="zero", align_bytes=64)
        nc.vector.memset(zero[:], 0.0)
        one = keep.tile([P, 1], F32, name="one")
        nc.scalar.activation(one[:], zero[:], ACT.Exp)

        scale_pool = keep.tile([P, POOL // 4], I32, name="scale_pool", tag="scale_pool", align_bytes=64)
        nc.vector.memset(scale_pool[0 : P - QUAD], 0)
        nc.sync.dma_start(scale_pool[P - QUAD : P], k_scales.rearrange("o f t -> f o t").bitcast(I32))
        kn_pool = keep.tile([P, POOL], F32, name="kn_pool", tag="kn_pool", align_bytes=64)
        bw_pool = keep.tile([P, POOL], F32, name="bw_pool", tag="bw_pool", align_bytes=64)
        nc.sync.dma_start(kn_pool[P - 1 : P, :], kn[0:1, :])
        nc.vector.memset(kn_pool[0 : P - 1, :].bitcast(I32), 0)
        nc.vector.memset(bw_pool[0 : P - 1, :].bitcast(I32), 0)

        k_scale = keep.tile([P, PASSES, SLOTS], U8, name="k_scale", align_bytes=64)
        nc.vector.memset(k_scale[:].rearrange("p o s -> p (o s)").bitcast(I32), 0)

        row_minus_column = keep.tile([P, P], I32, name="row_minus_column")
        nc.gpsimd.iota(row_minus_column[:], pattern=[[-1, P]], base=0, channel_multiplier=1)
        identity = keep.tile([P, P], F32, name="identity")
        nc.vector.tensor_scalar(identity[:], row_minus_column[:], 0.0, one[:], ALU.is_equal, ALU.mult)

        q_rows = qT[0].rearrange("(o p j) w -> o p j w", o=PASSES, j=PACK)

        def load_q(o, c0, width, tag):
            raw = keep.tile([P, PACK, width], F32, name="raw_%d_%d" % (o, c0), tag=tag, align_bytes=64)
            nc.sync.dma_start(raw[:], q_rows[o][:, :, c0 : c0 + width])
            return raw

        def quantize(raw, name, tag):
            width = raw.shape[2]
            grouped = keep.tile([P, width * PACK], BF16, name=name + "_grouped", tag=tag, align_bytes=64)
            nc.scalar.copy(
                grouped[:].rearrange("p (c i j) -> p c j i", i=LINE, j=PACK),
                raw[:].rearrange("p j (c i) -> p c j i", i=LINE),
            )
            codes = keep.tile([P, width], U32, name=name + "_codes", align_bytes=64)
            scales = keep.tile([P, width], U8, name=name + "_scales", align_bytes=64)
            nc.vector.quantize_mx(out=codes[:].bitcast(FP8X4), scales=scales[:], in_=grouped[:])
            return codes, scales

        (first0, first_width), (second0, second_width), (third0, third_width) = CHUNKS

        raw_first = [load_q(0, first0, first_width, "raw_first0")]
        nc.sync.dma_start(bw_pool[P - 1 : P, :], bw[0:1, :])
        qn_cols = keep.tile([P, PACK], F32, name="qn_cols")
        nc.sync.dma_start(qn_cols[:], qn[0, 0].rearrange("(p c) -> p c", c=PACK))
        raw_first.append(load_q(1, first0, first_width, "raw_first1"))
        word_pool = keep.tile([P, POOL], U32, name="word_pool")
        nc.sync.dma_start(word_pool[:].bitcast(I32), k_words[0].rearrange("p t b -> p (t b)").bitcast(I32))

        scale_rows = keep.tile([P, SLOTS], U8, name="scale_rows", align_bytes=64)
        nc.vector.tensor_copy(scale_rows[:], scale_pool[:].bitcast(U8).indirect(offsets[:]))
        rows_a_quad = PASSES * SCALE_ROWS
        for quad in range(P // QUAD):
            source = P - QUAD + rows_a_quad * quad
            nc.sync.dma_start(
                k_scale[QUAD * quad : QUAD * quad + SCALE_ROWS].rearrange("p o s -> p (o s)").bitcast(I32),
                scale_rows[source : source + rows_a_quad, :].bitcast(I32),
            )
        kn_listed = keep.tile([P, SLOTS], F32, name="kn_listed")
        nc.vector.tensor_copy(kn_listed[:], kn_pool[:].indirect(offsets[:]))
        bw_listed = keep.tile([P, SLOTS], F32, name="bw_listed")
        nc.vector.tensor_copy(bw_listed[:], bw_pool[:].indirect(offsets[:]))

        raw_rest0 = load_q(0, second0, second_width + third_width, "scale_pool")
        raw_second1 = load_q(1, second0, second_width, "kn_pool")
        raw_third1 = load_q(1, third0, third_width, "bw_pool")

        qn_t = psum.tile([P, PACK, P], F32, name="qn_t", tag="bank%d" % (BANKS - 3))
        kn_t = psum.tile([P, SLOT_TILES, P], F32, name="kn_t", tag="bank%d" % (BANKS - 2))
        bw_t = psum.tile([P, SLOT_TILES, P], F32, name="bw_t", tag="bank%d" % (BANKS - 1))
        for c in range(PACK):
            nc.tensor.transpose(qn_t[:, c, :], qn_cols[:, c : c + 1].to_broadcast([P, P]), identity[:])
        for s in range(SLOT_TILES):
            nc.tensor.transpose(kn_t[:, s, :], kn_listed[:, s * P : (s + 1) * P], identity[:])
        for s in range(SLOT_TILES):
            nc.tensor.transpose(bw_t[:, s, :], bw_listed[:, s * P : (s + 1) * P], identity[:])

        q_first = [quantize(raw_first[o], "first%d" % o, "first%d_grouped" % o) for o in range(PASSES)]

        terms = keep.tile([P, NQ + 2 * SLOT_TILES], F32, name="terms", tag="raw_first1", align_bytes=64)
        half_qn = terms[:, 0:NQ]
        half_kn = terms[:, NQ : NQ + SLOT_TILES]
        minus_two_bw = terms[:, NQ + SLOT_TILES :]
        nc.scalar.activation(
            half_qn.rearrange("p (n c) -> p n c", c=PACK),
            qn_t[:].rearrange("p c n -> p n c"),
            ACT.Identity,
            bias=zero[:],
            scale=0.5,
        )
        nc.scalar.activation(half_kn, kn_t[:, :, P - 1], ACT.Identity, bias=zero[:], scale=0.5)
        nc.scalar.activation(minus_two_bw, bw_t[:, :, P - 1], ACT.Identity, bias=zero[:], scale=-2.0)

        k_codes = []
        for h in range(SLOTS // HALF):
            pairs = keep.tile([P, HALF], U32, name="pairs_%d" % h)
            entries = offsets[:, h * HALF // LIST_ROWS : (h + 1) * HALF // LIST_ROWS]
            nc.vector.tensor_copy(pairs[:], word_pool[:].indirect(entries))
            parted = keep.tile([P, PASSES, 2 * HALF], U8, name="k_codes_%d" % h, align_bytes=64)
            nc.vector.tensor_copy(parted[:].bitcast(U16), pairs[:].bitcast(U16).rearrange("p (s o) -> p o s", o=PASSES))
            k_codes.append(parted)

        q_rest0 = quantize(raw_rest0, "rest0", "zero")
        q_second1 = quantize(raw_second1, "second1", "scale_pool")
        q_third1 = quantize(raw_third1, "third1", "kn_pool")
        moving = [
            [(q_first[0], 0), (q_first[1], 0)],
            [(q_rest0, 0), (q_second1, 0)],
            [(q_rest0, second_width), (q_third1, 0)],
        ]

        result_tags = ["bw_pool", "result_second", "result_third"]
        results = [
            keep.tile([P, SLOT_TILES, width], F32, name="result_%d" % c, tag=result_tags[c], align_bytes=64)
            for c, (c0, width) in enumerate(CHUNKS)
        ]
        first_tags = ["gap_first0", "zero", "scale_pool", "gap_first3"]
        gaps_first = [
            keep.tile([P, first_width], F32, name="gap_first%d" % s, tag=first_tags[s], align_bytes=64)
            for s in range(SLOT_TILES)
        ]
        gaps_second = keep.tile([P, SLOT_TILES, second_width], F32, name="gaps_second", tag="kn_pool", align_bytes=64)
        gaps_third = keep.tile([P, SLOT_TILES, third_width], F32, name="gaps_third")
        gaps = [
            [tile[:] for tile in gaps_first],
            [gaps_second[:, s, :] for s in range(SLOT_TILES)],
            [gaps_third[:, s, :] for s in range(SLOT_TILES)],
        ]

        units = [(c, s) for c in range(len(CHUNKS)) for s in range(SLOT_TILES)]
        out_tiles = out[0].rearrange("(s p) q -> p s q", p=P)

        def score(u):
            c, s = units[u]
            c0, width = CHUNKS[c]
            h, tile_in_half = divmod(s, HALF // P)
            acc = psum.tile([P, width], F32, name="acc", tag="bank%d" % (u % BANKS))
            for n0 in range(0, width, N_MM):
                for o in range(PASSES):
                    (codes, scales), base = moving[c][o]
                    nc.tensor.matmul_mx(
                        out=acc[:, n0 : n0 + N_MM],
                        lhsT=k_codes[h][:, o, 2 * tile_in_half * P : 2 * (tile_in_half + 1) * P].bitcast(FP4X4),
                        lhsT_scale=k_scale[:, o, s * P : (s + 1) * P],
                        rhs=codes[:, base + n0 : base + n0 + N_MM].bitcast(FP8X4),
                        rhs_scale=scales[:, base + n0 : base + n0 + N_MM],
                        start=(o == 0),
                        stop=(o == PASSES - 1),
                    )
            nc.vector.scalar_tensor_tensor(
                gaps[c][s], acc[:], half_kn[:, s : s + 1], half_qn[:, c0 : c0 + width], ALU.subtract, ALU.subtract
            )

        def finish(u):
            c, s = units[u]
            c0, width = CHUNKS[c]
            clipped = keep.tile([P, width], F32, name="clipped_%d" % u)
            if c == SCALAR_CLIP_CHUNK:
                nc.scalar.activation(clipped[:], gaps[c][s], ACT.Relu, scale=-1.0)
            else:
                nc.vector.tensor_scalar(clipped[:], gaps[c][s], 0.0, -1.0, ALU.min, ALU.mult)
            nc.scalar.activation(results[c][:, s, :], clipped[:], ACT.Exp, scale=minus_two_bw[:, s : s + 1])
            if (s + 1) % TILES_A_STORE == 0:
                s0 = s + 1 - TILES_A_STORE
                queue = nc.scalar if u == len(units) - 1 else nc.sync
                queue.dma_start(out_tiles[:, s0 : s + 1, c0 : c0 + width], results[c][:, s0 : s + 1, :])

        score(0)
        for u in range(1, len(units)):
            score(u)
            finish(u - 1)
        finish(len(units) - 1)
